import numpy as np
import ml_dtypes

BF16 = ml_dtypes.bfloat16


def bf(x):
    return np.asarray(x, np.float32).astype(BF16)


def f32(x):
    return np.asarray(x, np.float32)


def f64(x):
    return np.asarray(x).astype(np.float64)


def striped(idx):
    return np.tile(idx.reshape(-1, 16).T, (8, 1))


S, K, M, N, E, Q = 512, 128, 256, 192, 2, 96


def setup_inputs():
    return {"base": bf(np.random.standard_normal((M, S))), "x": bf(np.random.standard_normal((K, N))), "w": bf(np.random.standard_normal((E, K, M)) / np.sqrt(K)), "b": f32(0.5 * np.random.standard_normal((M, 1))), "offs": striped(np.random.permutation(S)[:N])}


def reference(base, x, w, b, offs):
    idx = offs[:16].T.reshape(-1)
    z = f64(base).copy()
    for e in range(E):
        z[:, idx[e * Q : (e + 1) * Q]] += f64(w)[e].T @ f64(x)[:, e * Q : (e + 1) * Q]
    return z + f64(b)

@@ -1,0 +1,65 @@
+import concourse.mybir as mybir
+from concourse.masks import make_identity
+
+BF16, F32, U16 = mybir.dt.bfloat16, mybir.dt.float32, mybir.dt.uint16
+
+P = 128
+S = 512
+N = 192
+E = 2
+Q = N // E
+M = 256
+BLOCKS = M // P
+QCOLS = Q // 16
+
+FLOPS = 2 * P * N * M
+
+
+def tile_scatter_matmul_kernel(tc, base, x, w, b, offs, out):
+    nc = tc.nc
+    with (
+        tc.tile_pool(name="held", bufs=1) as held,
+        tc.psum_pool(name="psum", bufs=1) as psum,
+    ):
+        offsets = held.tile([P, N // 16], U16, name="offsets")
+        nc.sync.dma_start(offsets[:], offs)
+
+        base_tiles = [held.tile([P, S], BF16, name=f"base{a}") for a in range(BLOCKS)]
+        nc.sync.dma_start(base_tiles[0][:], base[0:P, :])
+        nc.scalar.dma_start(base_tiles[1][:], base[P : 2 * P, :])
+
+        x_tile = held.tile([P, N], BF16, name="x_tile")
+        nc.sync.dma_start(x_tile[:], x)
+        w_tile = held.tile([P, E, M], BF16, name="w_tile")
+        nc.scalar.dma_start(w_tile[:], w.rearrange("e k m -> k e m"))
+
+        bias = held.tile([P, BLOCKS], F32, name="bias")
+        with nc.allow_non_contiguous_dma(reason="one float32 bias value to a partition"):
+            nc.scalar.dma_start(bias[:], b.rearrange("(a p) o -> p (a o)", p=P))
+
+        ident = held.tile([P, P], BF16, name="ident")
+        make_identity(nc, ident[:])
+
+        windows = [psum.tile([P, S], F32, name=f"window{a}") for a in range(BLOCKS)]
+        for a in range(BLOCKS):
+            nc.tensor.matmul(windows[a][:], ident[:], base_tiles[a][:], start=True, stop=False)
+
+        for a in range(BLOCKS):
+            for e in range(E):
+                nc.tensor.matmul(
+                    windows[a][:].indirect(offsets[:, e * QCOLS : (e + 1) * QCOLS]),
+                    w_tile[:, e, a * P : (a + 1) * P],
+                    x_tile[:, e * Q : (e + 1) * Q],
+                    start=False,
+                    stop=(e == E - 1),
+                )
+
+        result0 = held.tile([P, S], F32, name="result0")
+        nc.vector.tensor_scalar_add(result0[:], windows[0][:], bias[:, 0:1])
+        nc.sync.dma_start(out[0:P, :], result0[:])
+
+        result1 = held.tile([P, S], F32, name="result1")
+        nc.scalar.activation(
+            result1[:], windows[1][:], mybir.ActivationFunctionType.Identity, bias=bias[:, 1:2]
+        )
+        nc.scalar.dma_start(out[P : 2 * P, :], result1[:])

@@ -21,21 +21,21 @@ def tile_scatter_matmul_kernel(tc, base, x, w, b, offs, out):
         tc.tile_pool(name="held", bufs=1) as held,
         tc.psum_pool(name="psum", bufs=1) as psum,
     ):
-        offsets = held.tile([P, N // 16], U16, name="offsets")
-        nc.sync.dma_start(offsets[:], offs)
-
         base_tiles = [held.tile([P, S], BF16, name=f"base{a}") for a in range(BLOCKS)]
         nc.sync.dma_start(base_tiles[0][:], base[0:P, :])
         nc.scalar.dma_start(base_tiles[1][:], base[P : 2 * P, :])
+
+        bias = held.tile([P, BLOCKS], F32, name="bias")
+        with nc.allow_non_contiguous_dma(reason="one float32 bias value to a partition"):
+            nc.sync.dma_start(bias[:], b.rearrange("(a p) o -> p (a o)", p=P))
+
+        offsets = held.tile([P, N // 16], U16, name="offsets")
+        nc.sync.dma_start(offsets[:], offs)
 
         x_tile = held.tile([P, N], BF16, name="x_tile")
         nc.sync.dma_start(x_tile[:], x)
         w_tile = held.tile([P, E, M], BF16, name="w_tile")
         nc.scalar.dma_start(w_tile[:], w.rearrange("e k m -> k e m"))
-
-        bias = held.tile([P, BLOCKS], F32, name="bias")
-        with nc.allow_non_contiguous_dma(reason="one float32 bias value to a partition"):
-            nc.scalar.dma_start(bias[:], b.rearrange("(a p) o -> p (a o)", p=P))
 
         ident = held.tile([P, P], BF16, name="ident")
         make_identity(nc, ident[:])

@@ -12,6 +12,8 @@ M = 256
 BLOCKS = M // P
 QCOLS = Q // 16
 
+WARM_UPS = 12
+
 FLOPS = 2 * P * N * M
 
 
@@ -39,6 +41,15 @@ def tile_scatter_matmul_kernel(tc, base, x, w, b, offs, out):
 
         ident = held.tile([P, P], BF16, name="ident")
         make_identity(nc, ident[:])
+
+        zeros = held.tile([P, P], BF16, name="zeros")
+        nc.vector.memset(zeros[:], 0.0)
+        idle_bank = psum.tile([P, P], F32, name="idle_bank")
+        for i in range(WARM_UPS):
+            nc.tensor.matmul(idle_bank[:], zeros[:], zeros[:], start=True, stop=True)
+
+        scratch = held.tile([P, 1], F32, name="scratch")
+        nc.scalar.activation(scratch[:], zeros[:, 0:1], mybir.ActivationFunctionType.Identity)
 
         windows = [psum.tile([P, S], F32, name=f"window{a}") for a in range(BLOCKS)]
         for a in range(BLOCKS):

@@ -24,12 +24,8 @@ def tile_scatter_matmul_kernel(tc, base, x, w, b, offs, out):
         tc.psum_pool(name="psum", bufs=1) as psum,
     ):
         base_tiles = [held.tile([P, S], BF16, name=f"base{a}") for a in range(BLOCKS)]
-        nc.sync.dma_start(base_tiles[0][:], base[0:P, :])
-        nc.scalar.dma_start(base_tiles[1][:], base[P : 2 * P, :])
-
-        bias = held.tile([P, BLOCKS], F32, name="bias")
-        with nc.allow_non_contiguous_dma(reason="one float32 bias value to a partition"):
-            nc.sync.dma_start(bias[:], b.rearrange("(a p) o -> p (a o)", p=P))
+        for a in range(BLOCKS):
+            nc.sync.dma_start(base_tiles[a][:], base[a * P : (a + 1) * P, :])
 
         offsets = held.tile([P, N // 16], U16, name="offsets")
         nc.sync.dma_start(offsets[:], offs)
@@ -37,7 +33,11 @@ def tile_scatter_matmul_kernel(tc, base, x, w, b, offs, out):
         x_tile = held.tile([P, N], BF16, name="x_tile")
         nc.sync.dma_start(x_tile[:], x)
         w_tile = held.tile([P, E, M], BF16, name="w_tile")
-        nc.scalar.dma_start(w_tile[:], w.rearrange("e k m -> k e m"))
+        nc.sync.dma_start(w_tile[:], w.rearrange("e k m -> k e m"))
+
+        bias = held.tile([P, BLOCKS], F32, name="bias")
+        with nc.allow_non_contiguous_dma(reason="one float32 bias value to a partition"):
+            nc.sync.dma_start(bias[:], b.rearrange("(a p) o -> p (a o)", p=P))
 
         ident = held.tile([P, P], BF16, name="ident")
         make_identity(nc, ident[:])

@@ -73,4 +73,4 @@ def tile_scatter_matmul_kernel(tc, base, x, w, b, offs, out):
         nc.scalar.activation(
             result1[:], windows[1][:], mybir.ActivationFunctionType.Identity, bias=bias[:, 1:2]
         )
-        nc.scalar.dma_start(out[P : 2 * P, :], result1[:])
+        nc.sync.dma_start(out[P : 2 * P, :], result1[:])

@@ -23,17 +23,17 @@ def tile_scatter_matmul_kernel(tc, base, x, w, b, offs, out):
         tc.tile_pool(name="held", bufs=1) as held,
         tc.psum_pool(name="psum", bufs=1) as psum,
     ):
-        base_tiles = [held.tile([P, S], BF16, name=f"base{a}") for a in range(BLOCKS)]
-        for a in range(BLOCKS):
-            nc.sync.dma_start(base_tiles[a][:], base[a * P : (a + 1) * P, :])
+        base_tile = held.tile([P, BLOCKS, S], BF16, name="base_tile")
+        nc.sync.dma_start(base_tile[:], base.rearrange("(a p) t -> p a t", p=P))
 
         offsets = held.tile([P, N // 16], U16, name="offsets")
         nc.sync.dma_start(offsets[:], offs)
 
         x_tile = held.tile([P, N], BF16, name="x_tile")
         nc.sync.dma_start(x_tile[:], x)
-        w_tile = held.tile([P, E, M], BF16, name="w_tile")
-        nc.sync.dma_start(w_tile[:], w.rearrange("e k m -> k e m"))
+        w_tiles = [held.tile([P, M], BF16, name=f"w{e}") for e in range(E)]
+        for e in range(E):
+            nc.sync.dma_start(w_tiles[e][:], w[e, :, :])
 
         bias = held.tile([P, BLOCKS], F32, name="bias")
         with nc.allow_non_contiguous_dma(reason="one float32 bias value to a partition"):
@@ -53,13 +53,13 @@ def tile_scatter_matmul_kernel(tc, base, x, w, b, offs, out):
 
         windows = [psum.tile([P, S], F32, name=f"window{a}") for a in range(BLOCKS)]
         for a in range(BLOCKS):
-            nc.tensor.matmul(windows[a][:], ident[:], base_tiles[a][:], start=True, stop=False)
+            nc.tensor.matmul(windows[a][:], ident[:], base_tile[:, a, :], start=True, stop=False)
 
         for a in range(BLOCKS):
             for e in range(E):
                 nc.tensor.matmul(
                     windows[a][:].indirect(offsets[:, e * QCOLS : (e + 1) * QCOLS]),
-                    w_tile[:, e, a * P : (a + 1) * P],
+                    w_tiles[e][:, a * P : (a + 1) * P],
                     x_tile[:, e * Q : (e + 1) * Q],
                     start=False,
                     stop=(e == E - 1),

@@ -12,7 +12,7 @@ M = 256
 BLOCKS = M // P
 QCOLS = Q // 16
 
-WARM_UPS = 12
+WARM_UPS = 8
 
 FLOPS = 2 * P * N * M
 

import concourse.mybir as mybir
from concourse.masks import make_identity

BF16, F32, U16 = mybir.dt.bfloat16, mybir.dt.float32, mybir.dt.uint16

P = 128
S = 512
N = 192
E = 2
Q = N // E
M = 256
BLOCKS = M // P
QCOLS = Q // 16

WARM_UPS = 8

FLOPS = 2 * P * N * M


def tile_scatter_matmul_kernel(tc, base, x, w, b, offs, out):
    nc = tc.nc
    with (
        tc.tile_pool(name="held", bufs=1) as held,
        tc.psum_pool(name="psum", bufs=1) as psum,
    ):
        base_tile = held.tile([P, BLOCKS, S], BF16, name="base_tile")
        nc.sync.dma_start(base_tile[:], base.rearrange("(a p) t -> p a t", p=P))

        offsets = held.tile([P, N // 16], U16, name="offsets")
        nc.sync.dma_start(offsets[:], offs)

        x_tile = held.tile([P, N], BF16, name="x_tile")
        nc.sync.dma_start(x_tile[:], x)
        w_tiles = [held.tile([P, M], BF16, name=f"w{e}") for e in range(E)]
        for e in range(E):
            nc.sync.dma_start(w_tiles[e][:], w[e, :, :])

        bias = held.tile([P, BLOCKS], F32, name="bias")
        with nc.allow_non_contiguous_dma(reason="one float32 bias value to a partition"):
            nc.sync.dma_start(bias[:], b.rearrange("(a p) o -> p (a o)", p=P))

        ident = held.tile([P, P], BF16, name="ident")
        make_identity(nc, ident[:])

        zeros = held.tile([P, P], BF16, name="zeros")
        nc.vector.memset(zeros[:], 0.0)
        idle_bank = psum.tile([P, P], F32, name="idle_bank")
        for i in range(WARM_UPS):
            nc.tensor.matmul(idle_bank[:], zeros[:], zeros[:], start=True, stop=True)

        scratch = held.tile([P, 1], F32, name="scratch")
        nc.scalar.activation(scratch[:], zeros[:, 0:1], mybir.ActivationFunctionType.Identity)

        windows = [psum.tile([P, S], F32, name=f"window{a}") for a in range(BLOCKS)]
        for a in range(BLOCKS):
            nc.tensor.matmul(windows[a][:], ident[:], base_tile[:, a, :], start=True, stop=False)

        for a in range(BLOCKS):
            for e in range(E):
                nc.tensor.matmul(
                    windows[a][:].indirect(offsets[:, e * QCOLS : (e + 1) * QCOLS]),
                    w_tiles[e][:, a * P : (a + 1) * P],
                    x_tile[:, e * Q : (e + 1) * Q],
                    start=False,
                    stop=(e == E - 1),
                )

        result0 = held.tile([P, S], F32, name="result0")
        nc.vector.tensor_scalar_add(result0[:], windows[0][:], bias[:, 0:1])
        nc.sync.dma_start(out[0:P, :], result0[:])

        result1 = held.tile([P, S], F32, name="result1")
        nc.scalar.activation(
            result1[:], windows[1][:], mybir.ActivationFunctionType.Identity, bias=bias[:, 1:2]
        )
        nc.sync.dma_start(out[P : 2 * P, :], result1[:])
